import numpy as np
import ml_dtypes

BF16 = ml_dtypes.bfloat16


def bf(x):
    return np.asarray(x, np.float32).astype(BF16)


def f32(x):
    return np.asarray(x, np.float32)


def f64(x):
    return np.asarray(x).astype(np.float64)


def striped(idx):
    return np.tile(idx.reshape(-1, 16).T, (8, 1))


S, K, N, E, Q, H, O = 256, 512, 256, 2, 128, 256, 512


def setup_inputs():
    return {"table": bf(np.random.standard_normal((K, S))), "w": bf(np.random.standard_normal((E, K, H)) / np.sqrt(K)), "b": f32(0.5 * np.random.standard_normal((H, E))), "w2": bf(np.random.standard_normal((E, H, O)) / np.sqrt(H)), "offs": striped(np.sort(np.random.permutation(S).reshape(E, Q), axis=1).reshape(-1))}


def reference(table, w, b, w2, offs):
    idx = offs[:16].T.reshape(-1)
    x = f64(table)[:, idx]
    ys = []
    for e in range(E):
        t = f64(w)[e].T @ x[:, e * Q : (e + 1) * Q] + f64(b)[:, e : e + 1]
        t = np.maximum(t, 0.0)
        ys.append(f64(w2)[e].T @ t)
    return np.concatenate(ys, axis=1)

@@ -1,0 +1,74 @@
+import concourse.mybir as mybir
+
+P = 128
+S, K, H, O = 256, 512, 256, 512
+E, Q = 2, 128
+KB, HB, OB = K // P, H // P, O // P
+QC = Q // 16
+
+FLOPS = 2 * E * Q * (K * H + H * O)
+
+BF16, F32, U16 = mybir.dt.bfloat16, mybir.dt.float32, mybir.dt.uint16
+ADD, MAX = mybir.AluOpType.add, mybir.AluOpType.max
+
+
+def tile_rows_ffn2_relu_kernel(tc, table, w, b, w2, offs, out):
+    nc = tc.nc
+    with (
+        tc.tile_pool(name="held", bufs=1) as held,
+        tc.psum_pool(name="psum", bufs=1) as psum,
+    ):
+        offsets = held.tile([P, E * QC], U16, name="offsets")
+        nc.sync.dma_start(offsets[:], offs)
+
+        table_rows = table.rearrange("(p kb) s -> p kb s", kb=KB)
+        table_pairs = [held.tile([P, 2, S], BF16, name=f"table{t}") for t in range(KB // 2)]
+        w_tiles = [held.tile([P, KB, H], BF16, name=f"w{e}") for e in range(E)]
+        w2_tiles = [held.tile([P, HB, O], BF16, name=f"w2_{e}") for e in range(E)]
+        bias = held.tile([P, HB, E], F32, name="bias")
+
+        nc.scalar.dma_start(w_tiles[0][:], w[0].rearrange("(p kb) i -> p kb i", kb=KB))
+        for t in range(KB // 2):
+            nc.sync.dma_start(table_pairs[t][:], table_rows[:, 2 * t : 2 * t + 2, :])
+        nc.scalar.dma_start(bias[:], b.rearrange("(hb p) e -> p hb e", p=P))
+        nc.sync.dma_start(w_tiles[1][:], w[1].rearrange("(p kb) i -> p kb i", kb=KB))
+        for e in range(E):
+            nc.sync.dma_start(w2_tiles[e][:], w2[e].rearrange("(hb p) o -> p hb o", p=P))
+
+        hidden = [held.tile([P, HB, Q], BF16, name=f"hidden{e}") for e in range(E)]
+        for e in range(E):
+            picks = offsets[:, e * QC : (e + 1) * QC]
+            for hb in range(HB):
+                pre = psum.tile([P, Q], F32, name=f"pre{e}_{hb}")
+                for kb in range(KB):
+                    window = table_pairs[kb // 2][:, kb % 2, :]
+                    nc.tensor.matmul(
+                        pre[:],
+                        w_tiles[e][:, kb, hb * P : (hb + 1) * P],
+                        window.indirect(picks),
+                        start=(kb == 0),
+                        stop=(kb == KB - 1),
+                    )
+                nc.vector.tensor_scalar(
+                    hidden[e][:, hb, :], pre[:], bias[:, hb, e : e + 1], 0.0, ADD, MAX
+                )
+
+        sums = [psum.tile([P, E * Q], F32, name=f"sums{ob}") for ob in range(OB)]
+        for pair in range(OB // 2):
+            for e in range(E):
+                for ob in (2 * pair, 2 * pair + 1):
+                    for hb in range(HB):
+                        nc.tensor.matmul(
+                            sums[ob][:, e * Q : (e + 1) * Q],
+                            w2_tiles[e][:, hb, ob * P : (ob + 1) * P],
+                            hidden[e][:, hb, :],
+                            start=(hb == 0),
+                            stop=(hb == HB - 1),
+                        )
+            even, odd = 2 * pair, 2 * pair + 1
+            rows_even = held.tile([P, E * Q], F32, name=f"rows{even}")
+            nc.vector.tensor_copy(rows_even[:], sums[even][:])
+            nc.sync.dma_start(out[even * P : (even + 1) * P, :], rows_even[:])
+            rows_odd = held.tile([P, E * Q], F32, name=f"rows{odd}")
+            nc.scalar.copy(rows_odd[:], sums[odd][:])
+            nc.scalar.dma_start(out[odd * P : (odd + 1) * P, :], rows_odd[:])

@@ -5,6 +5,7 @@ S, K, H, O = 256, 512, 256, 512
 E, Q = 2, 128
 KB, HB, OB = K // P, H // P, O // P
 QC = Q // 16
+BANKS = 8
 
 FLOPS = 2 * E * Q * (K * H + H * O)
 
@@ -16,10 +17,9 @@ def tile_rows_ffn2_relu_kernel(tc, table, w, b, w2, offs, out):
     nc = tc.nc
     with (
         tc.tile_pool(name="held", bufs=1) as held,
-        tc.psum_pool(name="psum", bufs=1) as psum,
+        tc.psum_pool(name="psum", bufs=BANKS) as psum,
     ):
         offsets = held.tile([P, E * QC], U16, name="offsets")
-        nc.sync.dma_start(offsets[:], offs)
 
         table_rows = table.rearrange("(p kb) s -> p kb s", kb=KB)
         table_pairs = [held.tile([P, 2, S], BF16, name=f"table{t}") for t in range(KB // 2)]
@@ -27,48 +27,55 @@ def tile_rows_ffn2_relu_kernel(tc, table, w, b, w2, offs, out):
         w2_tiles = [held.tile([P, HB, O], BF16, name=f"w2_{e}") for e in range(E)]
         bias = held.tile([P, HB, E], F32, name="bias")
 
-        nc.scalar.dma_start(w_tiles[0][:], w[0].rearrange("(p kb) i -> p kb i", kb=KB))
+        w_rows = [w[e].rearrange("(p kb) i -> p kb i", kb=KB) for e in range(E)]
         for t in range(KB // 2):
-            nc.sync.dma_start(table_pairs[t][:], table_rows[:, 2 * t : 2 * t + 2, :])
+            nc.scalar.dma_start(
+                w_tiles[0][:, 2 * t : 2 * t + 2, :], w_rows[0][:, 2 * t : 2 * t + 2, :]
+            )
         nc.scalar.dma_start(bias[:], b.rearrange("(hb p) e -> p hb e", p=P))
-        nc.sync.dma_start(w_tiles[1][:], w[1].rearrange("(p kb) i -> p kb i", kb=KB))
+        nc.sync.dma_start(table_pairs[0][:], table_rows[:, 0:2, :])
+        nc.sync.dma_start(offsets[:], offs)
+        nc.sync.dma_start(table_pairs[1][:], table_rows[:, 2:4, :])
+        nc.sync.dma_start(w_tiles[1][:], w_rows[1])
         for e in range(E):
             nc.sync.dma_start(w2_tiles[e][:], w2[e].rearrange("(hb p) o -> p hb o", p=P))
 
         hidden = [held.tile([P, HB, Q], BF16, name=f"hidden{e}") for e in range(E)]
         for e in range(E):
             picks = offsets[:, e * QC : (e + 1) * QC]
+            pre = [psum.tile([P, Q], F32, name=f"pre{e}_{hb}", tag="bank") for hb in range(HB)]
+            for t in range(KB // 2):
+                for hb in range(HB):
+                    for half in range(2):
+                        kb = 2 * t + half
+                        nc.tensor.matmul(
+                            pre[hb][:],
+                            w_tiles[e][:, kb, hb * P : (hb + 1) * P],
+                            table_pairs[t][:, half, :].indirect(picks),
+                            start=(kb == 0),
+                            stop=(kb == KB - 1),
+                        )
             for hb in range(HB):
-                pre = psum.tile([P, Q], F32, name=f"pre{e}_{hb}")
-                for kb in range(KB):
-                    window = table_pairs[kb // 2][:, kb % 2, :]
-                    nc.tensor.matmul(
-                        pre[:],
-                        w_tiles[e][:, kb, hb * P : (hb + 1) * P],
-                        window.indirect(picks),
-                        start=(kb == 0),
-                        stop=(kb == KB - 1),
-                    )
                 nc.vector.tensor_scalar(
-                    hidden[e][:, hb, :], pre[:], bias[:, hb, e : e + 1], 0.0, ADD, MAX
+                    hidden[e][:, hb, :], pre[hb][:], bias[:, hb, e : e + 1], 0.0, ADD, MAX
                 )
 
-        sums = [psum.tile([P, E * Q], F32, name=f"sums{ob}") for ob in range(OB)]
-        for pair in range(OB // 2):
-            for e in range(E):
-                for ob in (2 * pair, 2 * pair + 1):
+        out_rows = out.rearrange("(ob p) j -> p ob j", p=P)
+        for e in range(E):
+            for pair in range(OB // 2):
+                staged = held.tile([P, 2, Q], F32, name=f"staged{e}_{pair}")
+                for side, evacuate in enumerate((nc.vector.tensor_copy, nc.scalar.copy)):
+                    ob = 2 * pair + side
+                    total = psum.tile([P, Q], F32, name=f"total{e}_{ob}", tag="bank")
                     for hb in range(HB):
                         nc.tensor.matmul(
-                            sums[ob][:, e * Q : (e + 1) * Q],
+                            total[:],
                             w2_tiles[e][:, hb, ob * P : (ob + 1) * P],
                             hidden[e][:, hb, :],
                             start=(hb == 0),
                             stop=(hb == HB - 1),
                         )
-            even, odd = 2 * pair, 2 * pair + 1
-            rows_even = held.tile([P, E * Q], F32, name=f"rows{even}")
-            nc.vector.tensor_copy(rows_even[:], sums[even][:])
-            nc.sync.dma_start(out[even * P : (even + 1) * P, :], rows_even[:])
-            rows_odd = held.tile([P, E * Q], F32, name=f"rows{odd}")
-            nc.scalar.copy(rows_odd[:], sums[odd][:])
-            nc.scalar.dma_start(out[odd * P : (odd + 1) * P, :], rows_odd[:])
+                    evacuate(staged[:, side, :], total[:])
+                nc.sync.dma_start(
+                    out_rows[:, 2 * pair : 2 * pair + 2, e * Q : (e + 1) * Q], staged[:]
+                )

@@ -6,6 +6,7 @@ E, Q = 2, 128
 KB, HB, OB = K // P, H // P, O // P
 QC = Q // 16
 BANKS = 8
+WARM_BLOCKS = 3
 
 FLOPS = 2 * E * Q * (K * H + H * O)
 
@@ -39,6 +40,17 @@ def tile_rows_ffn2_relu_kernel(tc, table, w, b, w2, offs, out):
         nc.sync.dma_start(w_tiles[1][:], w_rows[1])
         for e in range(E):
             nc.sync.dma_start(w2_tiles[e][:], w2[e].rearrange("(hb p) o -> p hb o", p=P))
+
+        zeros = held.tile([P, P], F32, name="zeros")
+        nc.vector.memset(zeros[:], 0.0)
+        unread = psum.tile([P, WARM_BLOCKS, P], F32, name="unread", tag="bank")
+        nc.tensor.matmul(
+            unread[:],
+            zeros[:],
+            zeros[:].unsqueeze(1).to_broadcast([P, WARM_BLOCKS, P]),
+            start=True,
+            stop=True,
+        )
 
         hidden = [held.tile([P, HB, Q], BF16, name=f"hidden{e}") for e in range(E)]
         for e in range(E):

@@ -5,6 +5,7 @@ S, K, H, O = 256, 512, 256, 512
 E, Q = 2, 128
 KB, HB, OB = K // P, H // P, O // P
 QC = Q // 16
+BIAS_PITCH = 8
 BANKS = 8
 WARM_BLOCKS = 3
 
@@ -26,18 +27,21 @@ def tile_rows_ffn2_relu_kernel(tc, table, w, b, w2, offs, out):
         table_pairs = [held.tile([P, 2, S], BF16, name=f"table{t}") for t in range(KB // 2)]
         w_tiles = [held.tile([P, KB, H], BF16, name=f"w{e}") for e in range(E)]
         w2_tiles = [held.tile([P, HB, O], BF16, name=f"w2_{e}") for e in range(E)]
-        bias = held.tile([P, HB, E], F32, name="bias")
+        bias = held.tile([P, HB, BIAS_PITCH], F32, name="bias")
 
         w_rows = [w[e].rearrange("(p kb) i -> p kb i", kb=KB) for e in range(E)]
         for t in range(KB // 2):
             nc.scalar.dma_start(
                 w_tiles[0][:, 2 * t : 2 * t + 2, :], w_rows[0][:, 2 * t : 2 * t + 2, :]
             )
-        nc.scalar.dma_start(bias[:], b.rearrange("(hb p) e -> p hb e", p=P))
+        nc.scalar.dma_start(bias[:, :, 0:E], b.rearrange("(hb p) e -> p hb e", p=P))
         nc.sync.dma_start(table_pairs[0][:], table_rows[:, 0:2, :])
         nc.sync.dma_start(offsets[:], offs)
         nc.sync.dma_start(table_pairs[1][:], table_rows[:, 2:4, :])
-        nc.sync.dma_start(w_tiles[1][:], w_rows[1])
+        for t in range(KB // 2):
+            nc.sync.dma_start(
+                w_tiles[1][:, 2 * t : 2 * t + 2, :], w_rows[1][:, 2 * t : 2 * t + 2, :]
+            )
         for e in range(E):
             nc.sync.dma_start(w2_tiles[e][:], w2[e].rearrange("(hb p) o -> p hb o", p=P))
 

@@ -30,20 +30,23 @@ def tile_rows_ffn2_relu_kernel(tc, table, w, b, w2, offs, out):
         bias = held.tile([P, HB, BIAS_PITCH], F32, name="bias")
 
         w_rows = [w[e].rearrange("(p kb) i -> p kb i", kb=KB) for e in range(E)]
+        nc.sync.dma_start(table_pairs[0][:], table_rows[:, 0:2, :])
+        nc.sync.dma_start(offsets[:], offs)
         for t in range(KB // 2):
             nc.scalar.dma_start(
                 w_tiles[0][:, 2 * t : 2 * t + 2, :], w_rows[0][:, 2 * t : 2 * t + 2, :]
             )
         nc.scalar.dma_start(bias[:, :, 0:E], b.rearrange("(hb p) e -> p hb e", p=P))
-        nc.sync.dma_start(table_pairs[0][:], table_rows[:, 0:2, :])
-        nc.sync.dma_start(offsets[:], offs)
         nc.sync.dma_start(table_pairs[1][:], table_rows[:, 2:4, :])
         for t in range(KB // 2):
             nc.sync.dma_start(
                 w_tiles[1][:, 2 * t : 2 * t + 2, :], w_rows[1][:, 2 * t : 2 * t + 2, :]
             )
         for e in range(E):
-            nc.sync.dma_start(w2_tiles[e][:], w2[e].rearrange("(hb p) o -> p hb o", p=P))
+            w2_rows = w2[e].rearrange("(hb p) o -> p hb o", p=P)
+            for pair in range(OB // 2):
+                columns = slice(2 * pair * P, 2 * (pair + 1) * P)
+                nc.sync.dma_start(w2_tiles[e][:, :, columns], w2_rows[:, :, columns])
 
         zeros = held.tile([P, P], F32, name="zeros")
         nc.vector.memset(zeros[:], 0.0)

import concourse.mybir as mybir

P = 128
S, K, H, O = 256, 512, 256, 512
E, Q = 2, 128
KB, HB, OB = K // P, H // P, O // P
QC = Q // 16
BIAS_PITCH = 8
BANKS = 8
WARM_BLOCKS = 3

FLOPS = 2 * E * Q * (K * H + H * O)

BF16, F32, U16 = mybir.dt.bfloat16, mybir.dt.float32, mybir.dt.uint16
ADD, MAX = mybir.AluOpType.add, mybir.AluOpType.max


def tile_rows_ffn2_relu_kernel(tc, table, w, b, w2, offs, out):
    nc = tc.nc
    with (
        tc.tile_pool(name="held", bufs=1) as held,
        tc.psum_pool(name="psum", bufs=BANKS) as psum,
    ):
        offsets = held.tile([P, E * QC], U16, name="offsets")

        table_rows = table.rearrange("(p kb) s -> p kb s", kb=KB)
        table_pairs = [held.tile([P, 2, S], BF16, name=f"table{t}") for t in range(KB // 2)]
        w_tiles = [held.tile([P, KB, H], BF16, name=f"w{e}") for e in range(E)]
        w2_tiles = [held.tile([P, HB, O], BF16, name=f"w2_{e}") for e in range(E)]
        bias = held.tile([P, HB, BIAS_PITCH], F32, name="bias")

        w_rows = [w[e].rearrange("(p kb) i -> p kb i", kb=KB) for e in range(E)]
        nc.sync.dma_start(table_pairs[0][:], table_rows[:, 0:2, :])
        nc.sync.dma_start(offsets[:], offs)
        for t in range(KB // 2):
            nc.scalar.dma_start(
                w_tiles[0][:, 2 * t : 2 * t + 2, :], w_rows[0][:, 2 * t : 2 * t + 2, :]
            )
        nc.scalar.dma_start(bias[:, :, 0:E], b.rearrange("(hb p) e -> p hb e", p=P))
        nc.sync.dma_start(table_pairs[1][:], table_rows[:, 2:4, :])
        for t in range(KB // 2):
            nc.sync.dma_start(
                w_tiles[1][:, 2 * t : 2 * t + 2, :], w_rows[1][:, 2 * t : 2 * t + 2, :]
            )
        for e in range(E):
            w2_rows = w2[e].rearrange("(hb p) o -> p hb o", p=P)
            for pair in range(OB // 2):
                columns = slice(2 * pair * P, 2 * (pair + 1) * P)
                nc.sync.dma_start(w2_tiles[e][:, :, columns], w2_rows[:, :, columns])

        zeros = held.tile([P, P], F32, name="zeros")
        nc.vector.memset(zeros[:], 0.0)
        unread = psum.tile([P, WARM_BLOCKS, P], F32, name="unread", tag="bank")
        nc.tensor.matmul(
            unread[:],
            zeros[:],
            zeros[:].unsqueeze(1).to_broadcast([P, WARM_BLOCKS, P]),
            start=True,
            stop=True,
        )

        hidden = [held.tile([P, HB, Q], BF16, name=f"hidden{e}") for e in range(E)]
        for e in range(E):
            picks = offsets[:, e * QC : (e + 1) * QC]
            pre = [psum.tile([P, Q], F32, name=f"pre{e}_{hb}", tag="bank") for hb in range(HB)]
            for t in range(KB // 2):
                for hb in range(HB):
                    for half in range(2):
                        kb = 2 * t + half
                        nc.tensor.matmul(
                            pre[hb][:],
                            w_tiles[e][:, kb, hb * P : (hb + 1) * P],
                            table_pairs[t][:, half, :].indirect(picks),
                            start=(kb == 0),
                            stop=(kb == KB - 1),
                        )
            for hb in range(HB):
                nc.vector.tensor_scalar(
                    hidden[e][:, hb, :], pre[hb][:], bias[:, hb, e : e + 1], 0.0, ADD, MAX
                )

        out_rows = out.rearrange("(ob p) j -> p ob j", p=P)
        for e in range(E):
            for pair in range(OB // 2):
                staged = held.tile([P, 2, Q], F32, name=f"staged{e}_{pair}")
                for side, evacuate in enumerate((nc.vector.tensor_copy, nc.scalar.copy)):
                    ob = 2 * pair + side
                    total = psum.tile([P, Q], F32, name=f"total{e}_{ob}", tag="bank")
                    for hb in range(HB):
                        nc.tensor.matmul(
                            total[:],
                            w2_tiles[e][:, hb, ob * P : (ob + 1) * P],
                            hidden[e][:, hb, :],
                            start=(hb == 0),
                            stop=(hb == HB - 1),
                        )
                    evacuate(staged[:, side, :], total[:])
                nc.sync.dma_start(
                    out_rows[:, 2 * pair : 2 * pair + 2, e * Q : (e + 1) * Q], staged[:]
                )
